import numpy as np
import ml_dtypes


def mxq(x, axis, fmt="e4m3"):
    dtype, down = {"e4m3": (ml_dtypes.float8_e4m3fn, 7), "e5m2": (ml_dtypes.float8_e5m2, 14)}[fmt]
    v = np.moveaxis(np.asarray(x, np.float32).astype(ml_dtypes.bfloat16).astype(np.float64), axis, -1)
    blocks = v.reshape(v.shape[:-1] + (-1, 32))
    amax = np.abs(blocks).max(-1, keepdims=True)
    byte = np.maximum(np.where(amax > 0, np.frexp(amax)[1] - 1 + 127, 0) - down, 1)
    scale = np.exp2(byte - 127.0)
    codes = (blocks / scale).astype(np.float32).astype(dtype).astype(np.float64)
    return np.moveaxis((codes * scale).reshape(v.shape), -1, axis)


WIDE = False


def mx_kscale(k):
    if not WIDE:
        return np.ones(k)
    levels = np.array([10, -10, 5, -5, 0])
    if k % 512:
        return np.exp2(np.random.permutation(np.resize(levels, k // 32))).repeat(32)
    a = np.empty((k // 512, 16))
    for p in range(k // 512):
        a[p, :8] = np.random.permutation(np.resize(levels, 8))
        for g in range(8):
            far = levels[np.abs(levels - a[p, g]) >= 10]
            a[p, g + 8] = far[np.random.randint(len(far))]
    return np.exp2(a.ravel()).repeat(32)


def f64(x):
    return np.asarray(x).astype(np.float64)


def striped(idx):
    return np.tile(np.asarray(idx).reshape(-1, 16).T, (8, 1)).astype(np.uint16)


def unstriped(offs):
    return offs[:16].T.reshape(-1).astype(np.int64)


E2M1 = np.array([0.0, 0.5, 1.0, 1.5, 2.0, 3.0, 4.0, 6.0, -0.0, -0.5, -1.0, -1.5, -2.0, -3.0, -4.0, -6.0])


def pack_weight(w, fmt):
    k, n = w.shape
    w = f64(np.asarray(w, np.float32).astype(ml_dtypes.bfloat16)).reshape(k // 32, 32, n)
    amax = np.abs(w).max(1)
    if fmt == "e4m3":
        byte = np.frexp(amax)[1] - 1 + 127 - 7
    else:
        mant, ex = np.frexp(amax / 6.0)
        byte = np.where(mant > 0.5, ex, ex - 1) + 127
    byte = np.clip(np.where(amax > 0, byte, 1), 1, 254)
    scaled = (w * np.exp2(127.0 - byte)[:, None, :]).reshape(k, n).astype(np.float32)
    by_word = np.ascontiguousarray(scaled.reshape(k // 512, 128, 4, n).transpose(0, 1, 3, 2))
    if fmt == "e4m3":
        words = by_word.astype(ml_dtypes.float8_e4m3fn).view(np.uint8)
    else:
        c = by_word.astype(ml_dtypes.float4_e2m1fn).view(np.uint8) & 0xF
        words = (c[..., 0::2] | (c[..., 1::2] << 4)).reshape(k // 512, 128, 2 * n)
    return np.ascontiguousarray(words), np.ascontiguousarray(byte.astype(np.uint8).reshape(k // 512, 16, n))


def unpack_weight(words, scales, fmt):
    g, _, n = scales.shape
    words = np.ascontiguousarray(words).reshape(g, 128, n, -1)
    if fmt == "e4m3":
        vals = words.view(ml_dtypes.float8_e4m3fn).astype(np.float64)
    else:
        nib = np.empty((g, 128, n, 4), np.uint8)
        nib[..., 0::2] = words & 0xF
        nib[..., 1::2] = words >> 4
        vals = E2M1[nib]
    vals = vals * np.repeat(np.exp2(scales.astype(np.float64) - 127.0), 8, axis=1)[..., None]
    return vals.transpose(0, 1, 3, 2).reshape(g * 512, n)


def bf(x):
    return np.asarray(x, np.float32).astype(ml_dtypes.bfloat16)


def planes(Y):
    r, m = Y.shape
    b = f64(bf(Y)).reshape(r // 32, 32, m)
    amax = np.abs(b).max(1)
    byte = np.clip(np.where(amax > 0, np.frexp(amax)[1] - 1 + 127 - 7, 1), 1, 254)
    codes = (b * np.exp2(127.0 - byte)[:, None, :]).reshape(r, m).astype(np.float32).astype(ml_dtypes.float8_e4m3fn).view(np.uint8)
    words = codes.reshape(r // 512, 128, 4, m).transpose(0, 1, 3, 2)
    return np.ascontiguousarray(words), np.ascontiguousarray(byte.astype(np.uint8).reshape(r // 512, 16, m))


K, T, J, N = 1024, 2048, 512, 512


def setup_inputs():
    n = np.random.standard_normal
    idx = np.random.permutation(T)[:J]
    fk = mx_kscale(K)
    wap = pack_weight(n((K, N)) * 1 / np.sqrt(K) * fk[:, None], "e2m1")
    wbp = pack_weight(n((K, N)) * np.random.uniform(0.3, 1.7, (K, 1)) / np.sqrt(K) * fk[:, None], "e4m3")
    return {
        "xt": (n((K, T)) * np.random.uniform(0.3, 1.7, (1, T)) / fk[:, None]).astype(np.float32),
        "wa_words": wap[0],
        "wa_scales": wap[1],
        "wb_words": wbp[0],
        "wb_scales": wbp[1],
        "gm": (np.random.uniform(0.5, 2.0, (1, N))).astype(np.float32),
        "offs": striped(idx),
    }


def reference(xt, wa_words, wa_scales, wb_words, wb_scales, gm, offs):
    idx = unstriped(offs)
    wau = unpack_weight(wa_words, wa_scales, "e2m1")
    wbu = unpack_weight(wb_words, wb_scales, "e4m3")
    xtidxq = mxq(f64(xt)[:, idx], 0, "e4m3")
    a = xtidxq.T @ wau
    b = xtidxq.T @ wbu
    ea = np.mean(np.square(a), axis=1, keepdims=True)
    eb = np.mean(np.square(b), axis=1, keepdims=True)
    y = (ea * a + eb * b) / (ea + eb + 0.01) * f64(gm)
    words, scales = planes(y)
    return y, words, scales

@@ -1,0 +1,176 @@
+from contextlib import ExitStack
+
+import concourse.mybir as mybir
+from concourse.masks import make_identity
+
+K, T, J, N = 1024, 2048, 512, 512
+EPS = 0.01
+FLOPS = 2 * 2 * K * J * N
+
+F32 = mybir.dt.float32
+BF16 = mybir.dt.bfloat16
+I32 = mybir.dt.int32
+U32 = mybir.dt.uint32
+U16 = mybir.dt.uint16
+U8 = mybir.dt.uint8
+FP8X4 = mybir.dt.float8_e4m3fn_x4
+FP4X4 = mybir.dt.float4_e2m1fn_x4
+ACT = mybir.ActivationFunctionType
+MULT = mybir.AluOpType.mult
+ADD = mybir.AluOpType.add
+
+P = 128
+PACK = 4
+PASSES = K // (P * PACK)
+QUADS = 4
+VECTOR_ENERGIES = 2
+SCALAR_COLS = 192
+
+
+def tile_moe_experts_mixed_by_energy_pl_kernel(
+    tc, xt, wa_words, wa_scales, wb_words, wb_scales, gm, offs, out_0, out_1, out_2
+):
+    nc = tc.nc
+    with ExitStack() as ctx:
+        keep = ctx.enter_context(tc.tile_pool(name="keep", bufs=1))
+        psum = ctx.enter_context(tc.psum_pool(name="psum", bufs=1))
+
+        offsets = keep.tile([P, J // 16], U16, name="offsets")
+        rows = [keep.tile([P, T], F32, name="rows%d" % i) for i in range(PASSES * PACK)]
+        gm_dealt = keep.tile([P, PACK], F32, name="gm_dealt")
+        wa = [keep.tile([P, 2 * N], U8, name="wa%d" % z, align_bytes=64) for z in range(PASSES)]
+        wb = [keep.tile([P, N], U32, name="wb%d" % z, align_bytes=64) for z in range(PASSES)]
+        wa_plane = keep.tile([P, PASSES, N], U8, name="wa_plane", align_bytes=64)
+        wb_plane = keep.tile([P, N], U8, name="wb_plane", align_bytes=64)
+        identity = keep.tile([P, P], F32, name="identity")
+
+        nc.gpsimd.memset(wa_plane[:].bitcast(I32), 0)
+        nc.gpsimd.memset(wb_plane[:].bitcast(I32), 0)
+        make_identity(nc, identity[:])
+
+        xt_rows = xt.rearrange("(z p r) t -> z r p t", z=PASSES, r=PACK)
+
+        def load_rows(i):
+            nc.sync.dma_start(out=rows[i][:], in_=xt_rows[i // PACK, i % PACK])
+
+        load_rows(0)
+        nc.sync.dma_start(offsets[:], offs)
+        nc.sync.dma_start(out=gm_dealt[:], in_=gm.rearrange("o (p c) -> (o p) c", c=PACK))
+        load_rows(1)
+        load_rows(2)
+        for q in range(QUADS):
+            nc.sync.dma_start(
+                out=wa_plane[32 * q : 32 * q + 4, :, :].bitcast(I32),
+                in_=wa_scales[:, 4 * q : 4 * q + 4, :].rearrange("z i n -> i z n").bitcast(I32),
+            )
+        for i in range(3, PASSES * PACK - 1):
+            load_rows(i)
+
+        def load_wa(z):
+            nc.sync.dma_start(out=wa[z][:].bitcast(I32), in_=wa_words[z].bitcast(I32))
+
+        def load_wb(z):
+            nc.sync.dma_start(
+                out=wb[z][:].bitcast(I32), in_=wb_words[z].rearrange("p n r -> p (n r)").bitcast(I32)
+            )
+
+        load_wa(0)
+        load_rows(PASSES * PACK - 1)
+        for q in range(QUADS):
+            nc.sync.dma_start(
+                out=wb_plane[32 * q + 4 : 32 * q + 4 + 4 * PASSES, :].bitcast(I32),
+                in_=wb_scales[:, 4 * q : 4 * q + 4, :].bitcast(I32),
+            )
+        load_wb(0)
+        load_wa(1)
+        load_wb(1)
+
+        spread = psum.tile([P, PACK, P], F32, name="spread", tag="b%d" % (PACK - 1))
+        for c in range(PACK):
+            nc.tensor.transpose(spread[:, c, :], gm_dealt[:, c : c + 1].to_broadcast([P, P]), identity[:])
+        gm_all = keep.tile([P, N], F32, name="gm_all")
+        nc.scalar.activation(
+            gm_all[:].rearrange("p (i c) -> p i c", c=PACK), spread[:].rearrange("p c i -> p i c"), ACT.Copy
+        )
+
+        a = [psum.tile([P, N], F32, name="a%d" % t, tag="a%d" % t) for t in range(PACK)]
+        b = [psum.tile([P, N], F32, name="b%d" % t, tag="b%d" % t) for t in range(PACK)]
+
+        for z in range(PASSES):
+            picked = keep.tile([P, PACK, P, PACK], BF16, name="picked%d" % z, align_bytes=64)
+            for r in range(PACK):
+                nc.vector.tensor_copy(
+                    picked[:, :, :, r].rearrange("p t m -> p m t"), rows[PACK * z + r][:].indirect(offsets[:])
+                )
+            for t in range(PACK):
+                codes = keep.tile([P, P], U32, name="codes%d_%d" % (z, t), align_bytes=64)
+                plane = keep.tile([P, P], U8, name="plane%d_%d" % (z, t), align_bytes=64)
+                nc.vector.quantize_mx(
+                    out=codes[:].bitcast(FP8X4), scales=plane[:], in_=picked[:, t].rearrange("p m r -> p (m r)")
+                )
+                nc.tensor.matmul_mx(
+                    out=a[t][:], lhsT=codes[:].bitcast(FP8X4), lhsT_scale=plane[:],
+                    rhs=wa[z][:].bitcast(FP4X4), rhs_scale=wa_plane[:, z, :],
+                    start=(z == 0), stop=(z == PASSES - 1),
+                )
+                nc.tensor.matmul_mx(
+                    out=b[t][:], lhsT=codes[:].bitcast(FP8X4), lhsT_scale=plane[:],
+                    rhs=wb[z][:].bitcast(FP8X4), rhs_scale=wb_plane[4 + 4 * z : P, :],
+                    start=(z == 0), stop=(z == PASSES - 1),
+                )
+
+        y = keep.tile([P, PACK, N], F32, name="y")
+        u = [keep.tile([P, N], F32, name="u%d" % t) for t in range(PACK)]
+        v = [keep.tile([P, N], F32, name="v%d" % t) for t in range(PACK)]
+        ea = [keep.tile([P, 1], F32, name="ea%d" % t) for t in range(PACK)]
+        eb = [keep.tile([P, 1], F32, name="eb%d" % t) for t in range(PACK)]
+        inv = [keep.tile([P, 1], F32, name="inv%d" % t) for t in range(PACK)]
+        y_rows = out_0.rearrange("(p t) n -> p t n", t=PACK)
+
+        def energy_scalar(bank, sink, e):
+            nc.scalar.activation(sink[:], bank[:], ACT.Square, scale=N ** -0.5, accum_out=e[:])
+
+        def energy_vector(bank, e, t):
+            stats = keep.tile([P, 6], F32, name="stats%d" % t)
+            moments = keep.tile([P, 2], F32, name="moments%d" % t)
+            nc.vector.bn_stats(stats[:], bank[:])
+            nc.vector.bn_aggr(moments[:], stats[:])
+            nc.vector.scalar_tensor_tensor(e[:], moments[:, 0:1], moments[:, 0:1], moments[:, 1:2], MULT, ADD)
+
+        for t in range(VECTOR_ENERGIES):
+            energy_vector(b[t], eb[t], t)
+        for t in range(PACK):
+            energy_scalar(a[t], u[t], ea[t])
+            if t >= VECTOR_ENERGIES:
+                energy_scalar(b[t], v[t], eb[t])
+            nc.scalar.activation(u[t][:], a[t][:], ACT.Copy, scale=ea[t][:])
+            den = keep.tile([P, 1], F32, name="den%d" % t)
+            nc.vector.tensor_scalar(den[:], ea[t][:], eb[t][:], EPS, ADD, ADD)
+            nc.vector.scalar_tensor_tensor(v[t][:], b[t][:], eb[t][:], u[t][:], MULT, ADD)
+            nc.vector.reciprocal(inv[t][:], den[:])
+            spans = [(0, N)] if t < PACK - 1 else [(0, SCALAR_COLS), (SCALAR_COLS, N)]
+            for c0, c1 in spans:
+                nc.vector.scalar_tensor_tensor(
+                    y[:, t, c0:c1], v[t][:, c0:c1], inv[t][:], gm_all[:, c0:c1], MULT, MULT
+                )
+            nc.sync.dma_start(out=y_rows[:, t, :], in_=y[:, t, :])
+
+        woven = keep.tile([P, N, PACK], BF16, name="woven", align_bytes=64)
+        nc.scalar.copy(woven[:, :SCALAR_COLS, :], y[:, :, :SCALAR_COLS].rearrange("p t n -> p n t"))
+        nc.vector.tensor_copy(woven[:, SCALAR_COLS:, :], y[:, :, SCALAR_COLS:].rearrange("p t n -> p n t"))
+        y_codes = keep.tile([P, N], U32, name="y_codes", align_bytes=64)
+        y_plane = keep.tile([P, N], U8, name="y_plane", align_bytes=64)
+        for c0, c1 in ((N // 2, N), (0, N // 2)):
+            nc.vector.quantize_mx(
+                out=y_codes[:, c0:c1].bitcast(FP8X4), scales=y_plane[:, c0:c1],
+                in_=woven[:, c0:c1, :].rearrange("p n t -> p (n t)"),
+            )
+            nc.sync.dma_start(
+                out=out_1[0][:, c0:c1, :].rearrange("p n r -> p (n r)").bitcast(I32),
+                in_=y_codes[:, c0:c1].bitcast(I32),
+            )
+        for q in range(QUADS):
+            queue = nc.sync if q % 2 == 0 else nc.scalar
+            queue.dma_start(
+                out=out_2[0, 4 * q : 4 * q + 4, :].bitcast(I32), in_=y_plane[32 * q : 32 * q + 4, :].bitcast(I32)
+            )

@@ -44,8 +44,8 @@ def tile_moe_experts_mixed_by_energy_pl_kernel(
         wb_plane = keep.tile([P, N], U8, name="wb_plane", align_bytes=64)
         identity = keep.tile([P, P], F32, name="identity")
 
-        nc.gpsimd.memset(wa_plane[:].bitcast(I32), 0)
-        nc.gpsimd.memset(wb_plane[:].bitcast(I32), 0)
+        nc.vector.memset(wa_plane[:].bitcast(I32), 0)
+        nc.vector.memset(wb_plane[:].bitcast(I32), 0)
         make_identity(nc, identity[:])
 
         xt_rows = xt.rearrange("(z p r) t -> z r p t", z=PASSES, r=PACK)
@@ -55,15 +55,13 @@ def tile_moe_experts_mixed_by_energy_pl_kernel(
 
         load_rows(0)
         nc.sync.dma_start(offsets[:], offs)
-        nc.sync.dma_start(out=gm_dealt[:], in_=gm.rearrange("o (p c) -> (o p) c", c=PACK))
-        load_rows(1)
-        load_rows(2)
+        nc.scalar.dma_start(out=gm_dealt[:], in_=gm.rearrange("o (p c) -> (o p) c", c=PACK))
         for q in range(QUADS):
-            nc.sync.dma_start(
+            nc.scalar.dma_start(
                 out=wa_plane[32 * q : 32 * q + 4, :, :].bitcast(I32),
                 in_=wa_scales[:, 4 * q : 4 * q + 4, :].rearrange("z i n -> i z n").bitcast(I32),
             )
-        for i in range(3, PASSES * PACK - 1):
+        for i in range(1, PASSES * PACK - 1):
             load_rows(i)
 
         def load_wa(z):
@@ -98,7 +96,15 @@ def tile_moe_experts_mixed_by_energy_pl_kernel(
 
         for z in range(PASSES):
             picked = keep.tile([P, PACK, P, PACK], BF16, name="picked%d" % z, align_bytes=64)
-            for r in range(PACK):
+            dense_rows = PACK if z < PASSES - 1 else 2
+            dense = keep.tile([P, dense_rows, J], F32, name="dense%d" % z)
+            for r in range(dense_rows):
+                nc.vector.tensor_copy(dense[:, r, :], rows[PACK * z + r][:].indirect(offsets[:]))
+            nc.scalar.copy(
+                picked[:, :, :, :dense_rows].rearrange("p t m r -> p m t r"),
+                dense[:].rearrange("p r (m t) -> p m t r", t=PACK),
+            )
+            for r in range(dense_rows, PACK):
                 nc.vector.tensor_copy(
                     picked[:, :, :, r].rearrange("p t m -> p m t"), rows[PACK * z + r][:].indirect(offsets[:])
                 )
@@ -122,45 +128,80 @@ def tile_moe_experts_mixed_by_energy_pl_kernel(
         y = keep.tile([P, PACK, N], F32, name="y")
         u = [keep.tile([P, N], F32, name="u%d" % t) for t in range(PACK)]
         v = [keep.tile([P, N], F32, name="v%d" % t) for t in range(PACK)]
-        ea = [keep.tile([P, 1], F32, name="ea%d" % t) for t in range(PACK)]
-        eb = [keep.tile([P, 1], F32, name="eb%d" % t) for t in range(PACK)]
-        inv = [keep.tile([P, 1], F32, name="inv%d" % t) for t in range(PACK)]
+        ea = [keep.tile([P, 2], F32, name="ea%d" % h) for h in range(2)]
+        eb = [keep.tile([P, 2], F32, name="eb%d" % h) for h in range(2)]
+        den = [keep.tile([P, 2], F32, name="den%d" % h) for h in range(2)]
+        inv = [keep.tile([P, 2], F32, name="inv%d" % h) for h in range(2)]
         y_rows = out_0.rearrange("(p t) n -> p t n", t=PACK)
+        H = N // 2
+
+        def col(tiles, t):
+            return tiles[t // 2][:, t % 2 : t % 2 + 1]
 
         def energy_scalar(bank, sink, e):
-            nc.scalar.activation(sink[:], bank[:], ACT.Square, scale=N ** -0.5, accum_out=e[:])
+            nc.scalar.activation(sink[:], bank[:], ACT.Square, scale=N ** -0.5, accum_out=e)
 
-        def energy_vector(bank, e, t):
-            stats = keep.tile([P, 6], F32, name="stats%d" % t)
-            moments = keep.tile([P, 2], F32, name="moments%d" % t)
-            nc.vector.bn_stats(stats[:], bank[:])
-            nc.vector.bn_aggr(moments[:], stats[:])
-            nc.vector.scalar_tensor_tensor(e[:], moments[:, 0:1], moments[:, 0:1], moments[:, 1:2], MULT, ADD)
-
-        for t in range(VECTOR_ENERGIES):
-            energy_vector(b[t], eb[t], t)
+        stats = [keep.tile([P, 6], F32, name="stats%d" % t) for t in range(2)]
+        moments = [keep.tile([P, 2], F32, name="moments%d" % t) for t in range(2)]
+        for t in range(2):
+            nc.vector.bn_stats(stats[t][:], b[t][:])
+        for t in range(2):
+            nc.vector.bn_aggr(moments[t][:], stats[t][:])
+        for t in range(2):
+            mean, var = moments[t][:, 0:1], moments[t][:, 1:2]
+            nc.vector.scalar_tensor_tensor(col(eb, t), mean, mean, var, MULT, ADD)
         for t in range(PACK):
-            energy_scalar(a[t], u[t], ea[t])
-            if t >= VECTOR_ENERGIES:
-                energy_scalar(b[t], v[t], eb[t])
-            nc.scalar.activation(u[t][:], a[t][:], ACT.Copy, scale=ea[t][:])
-            den = keep.tile([P, 1], F32, name="den%d" % t)
-            nc.vector.tensor_scalar(den[:], ea[t][:], eb[t][:], EPS, ADD, ADD)
-            nc.vector.scalar_tensor_tensor(v[t][:], b[t][:], eb[t][:], u[t][:], MULT, ADD)
-            nc.vector.reciprocal(inv[t][:], den[:])
-            spans = [(0, N)] if t < PACK - 1 else [(0, SCALAR_COLS), (SCALAR_COLS, N)]
-            for c0, c1 in spans:
-                nc.vector.scalar_tensor_tensor(
-                    y[:, t, c0:c1], v[t][:, c0:c1], inv[t][:], gm_all[:, c0:c1], MULT, MULT
-                )
+            energy_scalar(a[t], u[t], col(ea, t))
+            if t >= 2:
+                energy_scalar(b[t], v[t], col(eb, t))
+            for c0, c1 in [(0, N)] if t < PACK - 1 else [(0, H), (H, N)]:
+                nc.scalar.activation(u[t][:, c0:c1], a[t][:, c0:c1], ACT.Copy, scale=col(ea, t))
+
+        def mix(t, c0, c1):
+            nc.vector.scalar_tensor_tensor(
+                v[t][:, c0:c1], b[t][:, c0:c1], col(eb, t), u[t][:, c0:c1], MULT, ADD
+            )
+
+        def share(t):
+            nc.vector.tensor_scalar(col(den, t), col(ea, t), col(eb, t), EPS, ADD, ADD)
+
+        def finish(t, c0, c1):
+            nc.vector.scalar_tensor_tensor(
+                y[:, t, c0:c1], v[t][:, c0:c1], col(inv, t), gm_all[:, c0:c1], MULT, MULT
+            )
+
+        def store(t):
             nc.sync.dma_start(out=y_rows[:, t, :], in_=y[:, t, :])
 
+        mix(0, 0, N)
+        nc.vector.scalar_tensor_tensor(den[0][:], ea[0][:], EPS, eb[0][:], ADD, ADD)
+        mix(1, 0, N)
+        nc.vector.reciprocal(inv[0][:], den[0][:])
+        finish(0, 0, N)
+        store(0)
+        share(2)
+        finish(1, 0, N)
+        store(1)
+        nc.vector.reciprocal(col(inv, 2), col(den, 2))
+        mix(2, 0, N)
+        share(3)
+        finish(2, 0, N)
+        store(2)
+        nc.vector.reciprocal(col(inv, 3), col(den, 3))
+        mix(3, 0, H)
+        mix(3, H, N)
+        finish(3, 0, H)
+        finish(3, H, N)
+        store(3)
+
         woven = keep.tile([P, N, PACK], BF16, name="woven", align_bytes=64)
-        nc.scalar.copy(woven[:, :SCALAR_COLS, :], y[:, :, :SCALAR_COLS].rearrange("p t n -> p n t"))
-        nc.vector.tensor_copy(woven[:, SCALAR_COLS:, :], y[:, :, SCALAR_COLS:].rearrange("p t n -> p n t"))
+        for c0, c1 in ((0, N // 4), (N // 4, SCALAR_COLS)):
+            nc.scalar.copy(woven[:, c0:c1, :], y[:, :, c0:c1].rearrange("p t n -> p n t"))
+        for c0, c1 in ((SCALAR_COLS, H), (H, N)):
+            nc.vector.tensor_copy(woven[:, c0:c1, :], y[:, :, c0:c1].rearrange("p t n -> p n t"))
         y_codes = keep.tile([P, N], U32, name="y_codes", align_bytes=64)
         y_plane = keep.tile([P, N], U8, name="y_plane", align_bytes=64)
-        for c0, c1 in ((N // 2, N), (0, N // 2)):
+        for c0, c1 in ((0, N // 4), (N // 2, N), (N // 4, N // 2)):
             nc.vector.quantize_mx(
                 out=y_codes[:, c0:c1].bitcast(FP8X4), scales=y_plane[:, c0:c1],
                 in_=woven[:, c0:c1, :].rearrange("p n t -> p (n t)"),

from contextlib import ExitStack

import concourse.mybir as mybir
from concourse.masks import make_identity

K, T, J, N = 1024, 2048, 512, 512
EPS = 0.01
FLOPS = 2 * 2 * K * J * N

F32 = mybir.dt.float32
BF16 = mybir.dt.bfloat16
I32 = mybir.dt.int32
U32 = mybir.dt.uint32
U16 = mybir.dt.uint16
U8 = mybir.dt.uint8
FP8X4 = mybir.dt.float8_e4m3fn_x4
FP4X4 = mybir.dt.float4_e2m1fn_x4
ACT = mybir.ActivationFunctionType
MULT = mybir.AluOpType.mult
ADD = mybir.AluOpType.add

P = 128
PACK = 4
PASSES = K // (P * PACK)
QUADS = 4
VECTOR_ENERGIES = 2
SCALAR_COLS = 192


def tile_moe_experts_mixed_by_energy_pl_kernel(
    tc, xt, wa_words, wa_scales, wb_words, wb_scales, gm, offs, out_0, out_1, out_2
):
    nc = tc.nc
    with ExitStack() as ctx:
        keep = ctx.enter_context(tc.tile_pool(name="keep", bufs=1))
        psum = ctx.enter_context(tc.psum_pool(name="psum", bufs=1))

        offsets = keep.tile([P, J // 16], U16, name="offsets")
        rows = [keep.tile([P, T], F32, name="rows%d" % i) for i in range(PASSES * PACK)]
        gm_dealt = keep.tile([P, PACK], F32, name="gm_dealt")
        wa = [keep.tile([P, 2 * N], U8, name="wa%d" % z, align_bytes=64) for z in range(PASSES)]
        wb = [keep.tile([P, N], U32, name="wb%d" % z, align_bytes=64) for z in range(PASSES)]
        wa_plane = keep.tile([P, PASSES, N], U8, name="wa_plane", align_bytes=64)
        wb_plane = keep.tile([P, N], U8, name="wb_plane", align_bytes=64)
        identity = keep.tile([P, P], F32, name="identity")

        nc.vector.memset(wa_plane[:].bitcast(I32), 0)
        nc.vector.memset(wb_plane[:].bitcast(I32), 0)
        make_identity(nc, identity[:])

        xt_rows = xt.rearrange("(z p r) t -> z r p t", z=PASSES, r=PACK)

        def load_rows(i):
            nc.sync.dma_start(out=rows[i][:], in_=xt_rows[i // PACK, i % PACK])

        load_rows(0)
        nc.sync.dma_start(offsets[:], offs)
        nc.scalar.dma_start(out=gm_dealt[:], in_=gm.rearrange("o (p c) -> (o p) c", c=PACK))
        for q in range(QUADS):
            nc.scalar.dma_start(
                out=wa_plane[32 * q : 32 * q + 4, :, :].bitcast(I32),
                in_=wa_scales[:, 4 * q : 4 * q + 4, :].rearrange("z i n -> i z n").bitcast(I32),
            )
        for i in range(1, PASSES * PACK - 1):
            load_rows(i)

        def load_wa(z):
            nc.sync.dma_start(out=wa[z][:].bitcast(I32), in_=wa_words[z].bitcast(I32))

        def load_wb(z):
            nc.sync.dma_start(
                out=wb[z][:].bitcast(I32), in_=wb_words[z].rearrange("p n r -> p (n r)").bitcast(I32)
            )

        load_wa(0)
        load_rows(PASSES * PACK - 1)
        for q in range(QUADS):
            nc.sync.dma_start(
                out=wb_plane[32 * q + 4 : 32 * q + 4 + 4 * PASSES, :].bitcast(I32),
                in_=wb_scales[:, 4 * q : 4 * q + 4, :].bitcast(I32),
            )
        load_wb(0)
        load_wa(1)
        load_wb(1)

        spread = psum.tile([P, PACK, P], F32, name="spread", tag="b%d" % (PACK - 1))
        for c in range(PACK):
            nc.tensor.transpose(spread[:, c, :], gm_dealt[:, c : c + 1].to_broadcast([P, P]), identity[:])
        gm_all = keep.tile([P, N], F32, name="gm_all")
        nc.scalar.activation(
            gm_all[:].rearrange("p (i c) -> p i c", c=PACK), spread[:].rearrange("p c i -> p i c"), ACT.Copy
        )

        a = [psum.tile([P, N], F32, name="a%d" % t, tag="a%d" % t) for t in range(PACK)]
        b = [psum.tile([P, N], F32, name="b%d" % t, tag="b%d" % t) for t in range(PACK)]

        for z in range(PASSES):
            picked = keep.tile([P, PACK, P, PACK], BF16, name="picked%d" % z, align_bytes=64)
            dense_rows = PACK if z < PASSES - 1 else 2
            dense = keep.tile([P, dense_rows, J], F32, name="dense%d" % z)
            for r in range(dense_rows):
                nc.vector.tensor_copy(dense[:, r, :], rows[PACK * z + r][:].indirect(offsets[:]))
            nc.scalar.copy(
                picked[:, :, :, :dense_rows].rearrange("p t m r -> p m t r"),
                dense[:].rearrange("p r (m t) -> p m t r", t=PACK),
            )
            for r in range(dense_rows, PACK):
                nc.vector.tensor_copy(
                    picked[:, :, :, r].rearrange("p t m -> p m t"), rows[PACK * z + r][:].indirect(offsets[:])
                )
            for t in range(PACK):
                codes = keep.tile([P, P], U32, name="codes%d_%d" % (z, t), align_bytes=64)
                plane = keep.tile([P, P], U8, name="plane%d_%d" % (z, t), align_bytes=64)
                nc.vector.quantize_mx(
                    out=codes[:].bitcast(FP8X4), scales=plane[:], in_=picked[:, t].rearrange("p m r -> p (m r)")
                )
                nc.tensor.matmul_mx(
                    out=a[t][:], lhsT=codes[:].bitcast(FP8X4), lhsT_scale=plane[:],
                    rhs=wa[z][:].bitcast(FP4X4), rhs_scale=wa_plane[:, z, :],
                    start=(z == 0), stop=(z == PASSES - 1),
                )
                nc.tensor.matmul_mx(
                    out=b[t][:], lhsT=codes[:].bitcast(FP8X4), lhsT_scale=plane[:],
                    rhs=wb[z][:].bitcast(FP8X4), rhs_scale=wb_plane[4 + 4 * z : P, :],
                    start=(z == 0), stop=(z == PASSES - 1),
                )

        y = keep.tile([P, PACK, N], F32, name="y")
        u = [keep.tile([P, N], F32, name="u%d" % t) for t in range(PACK)]
        v = [keep.tile([P, N], F32, name="v%d" % t) for t in range(PACK)]
        ea = [keep.tile([P, 2], F32, name="ea%d" % h) for h in range(2)]
        eb = [keep.tile([P, 2], F32, name="eb%d" % h) for h in range(2)]
        den = [keep.tile([P, 2], F32, name="den%d" % h) for h in range(2)]
        inv = [keep.tile([P, 2], F32, name="inv%d" % h) for h in range(2)]
        y_rows = out_0.rearrange("(p t) n -> p t n", t=PACK)
        H = N // 2

        def col(tiles, t):
            return tiles[t // 2][:, t % 2 : t % 2 + 1]

        def energy_scalar(bank, sink, e):
            nc.scalar.activation(sink[:], bank[:], ACT.Square, scale=N ** -0.5, accum_out=e)

        stats = [keep.tile([P, 6], F32, name="stats%d" % t) for t in range(2)]
        moments = [keep.tile([P, 2], F32, name="moments%d" % t) for t in range(2)]
        for t in range(2):
            nc.vector.bn_stats(stats[t][:], b[t][:])
        for t in range(2):
            nc.vector.bn_aggr(moments[t][:], stats[t][:])
        for t in range(2):
            mean, var = moments[t][:, 0:1], moments[t][:, 1:2]
            nc.vector.scalar_tensor_tensor(col(eb, t), mean, mean, var, MULT, ADD)
        for t in range(PACK):
            energy_scalar(a[t], u[t], col(ea, t))
            if t >= 2:
                energy_scalar(b[t], v[t], col(eb, t))
            for c0, c1 in [(0, N)] if t < PACK - 1 else [(0, H), (H, N)]:
                nc.scalar.activation(u[t][:, c0:c1], a[t][:, c0:c1], ACT.Copy, scale=col(ea, t))

        def mix(t, c0, c1):
            nc.vector.scalar_tensor_tensor(
                v[t][:, c0:c1], b[t][:, c0:c1], col(eb, t), u[t][:, c0:c1], MULT, ADD
            )

        def share(t):
            nc.vector.tensor_scalar(col(den, t), col(ea, t), col(eb, t), EPS, ADD, ADD)

        def finish(t, c0, c1):
            nc.vector.scalar_tensor_tensor(
                y[:, t, c0:c1], v[t][:, c0:c1], col(inv, t), gm_all[:, c0:c1], MULT, MULT
            )

        def store(t):
            nc.sync.dma_start(out=y_rows[:, t, :], in_=y[:, t, :])

        mix(0, 0, N)
        nc.vector.scalar_tensor_tensor(den[0][:], ea[0][:], EPS, eb[0][:], ADD, ADD)
        mix(1, 0, N)
        nc.vector.reciprocal(inv[0][:], den[0][:])
        finish(0, 0, N)
        store(0)
        share(2)
        finish(1, 0, N)
        store(1)
        nc.vector.reciprocal(col(inv, 2), col(den, 2))
        mix(2, 0, N)
        share(3)
        finish(2, 0, N)
        store(2)
        nc.vector.reciprocal(col(inv, 3), col(den, 3))
        mix(3, 0, H)
        mix(3, H, N)
        finish(3, 0, H)
        finish(3, H, N)
        store(3)

        woven = keep.tile([P, N, PACK], BF16, name="woven", align_bytes=64)
        for c0, c1 in ((0, N // 4), (N // 4, SCALAR_COLS)):
            nc.scalar.copy(woven[:, c0:c1, :], y[:, :, c0:c1].rearrange("p t n -> p n t"))
        for c0, c1 in ((SCALAR_COLS, H), (H, N)):
            nc.vector.tensor_copy(woven[:, c0:c1, :], y[:, :, c0:c1].rearrange("p t n -> p n t"))
        y_codes = keep.tile([P, N], U32, name="y_codes", align_bytes=64)
        y_plane = keep.tile([P, N], U8, name="y_plane", align_bytes=64)
        for c0, c1 in ((0, N // 4), (N // 2, N), (N // 4, N // 2)):
            nc.vector.quantize_mx(
                out=y_codes[:, c0:c1].bitcast(FP8X4), scales=y_plane[:, c0:c1],
                in_=woven[:, c0:c1, :].rearrange("p n t -> p (n t)"),
            )
            nc.sync.dma_start(
                out=out_1[0][:, c0:c1, :].rearrange("p n r -> p (n r)").bitcast(I32),
                in_=y_codes[:, c0:c1].bitcast(I32),
            )
        for q in range(QUADS):
            queue = nc.sync if q % 2 == 0 else nc.scalar
            queue.dma_start(
                out=out_2[0, 4 * q : 4 * q + 4, :].bitcast(I32), in_=y_plane[32 * q : 32 * q + 4, :].bitcast(I32)
            )
